import numpy as np
import ml_dtypes


def mxq(x, axis, fmt="e4m3"):
    dtype, down = {"e4m3": (ml_dtypes.float8_e4m3fn, 7), "e5m2": (ml_dtypes.float8_e5m2, 14)}[fmt]
    v = np.moveaxis(np.asarray(x, np.float32).astype(ml_dtypes.bfloat16).astype(np.float64), axis, -1)
    blocks = v.reshape(v.shape[:-1] + (-1, 32))
    amax = np.abs(blocks).max(-1, keepdims=True)
    byte = np.maximum(np.where(amax > 0, np.frexp(amax)[1] - 1 + 127, 0) - down, 1)
    scale = np.exp2(byte - 127.0)
    codes = (blocks / scale).astype(np.float32).astype(dtype).astype(np.float64)
    return np.moveaxis((codes * scale).reshape(v.shape), -1, axis)


WIDE = False


def mx_kscale(k):
    if not WIDE:
        return np.ones(k)
    levels = np.array([10, -10, 5, -5, 0])
    if k % 512:
        return np.exp2(np.random.permutation(np.resize(levels, k // 32))).repeat(32)
    a = np.empty((k // 512, 16))
    for p in range(k // 512):
        a[p, :8] = np.random.permutation(np.resize(levels, 8))
        for g in range(8):
            far = levels[np.abs(levels - a[p, g]) >= 10]
            a[p, g + 8] = far[np.random.randint(len(far))]
    return np.exp2(a.ravel()).repeat(32)


def f64(x):
    return np.asarray(x).astype(np.float64)


def striped(idx):
    return np.tile(idx.reshape(-1, 16).T, (8, 1)).astype(np.uint16)


def unstriped(offs):
    return offs[:16].T.reshape(-1).astype(np.int64)


def pack_weight(w):
    k, n = w.shape
    w = f64(np.asarray(w, np.float32).astype(ml_dtypes.bfloat16)).reshape(k // 32, 32, n)
    amax = np.abs(w).max(1)
    byte = np.clip(np.where(amax > 0, np.frexp(amax)[1] - 1 + 127 - 7, 1), 1, 254)
    scaled = (w * np.exp2(127.0 - byte)[:, None, :]).reshape(k, n).astype(np.float32)
    words = np.ascontiguousarray(scaled.reshape(k // 512, 128, 4, n).transpose(0, 1, 3, 2)).astype(ml_dtypes.float8_e4m3fn).view(np.uint8)
    return words, np.ascontiguousarray(byte.astype(np.uint8).reshape(k // 512, 16, n))


def unpack_weight(words, scales):
    g, p, n, _ = words.shape
    vals = np.ascontiguousarray(words).view(ml_dtypes.float8_e4m3fn).astype(np.float64) * np.repeat(np.exp2(scales.astype(np.float64) - 127.0), 8, axis=1)[..., None]
    return vals.transpose(0, 1, 3, 2).reshape(g * 512, n)


def gelu(v):
    return 0.5 * v * (1.0 + np.tanh(np.sqrt(2.0 / np.pi) * (v + 0.044715 * v**3)))


K, T, D, S, V, N = 1024, 2048, 3, 768, 256, 512
P = 2 ** 7


def setup_inputs():
    n = np.random.standard_normal
    s = mx_kscale(K)[:, None]
    words, scales = pack_weight(n((K, N)) / np.sqrt(K) / s)
    return {
        "xT": (n((K, T)) * s / np.sqrt(D)).astype(ml_dtypes.bfloat16).astype(np.float32),
        "w_words": words,
        "w_scales": scales,
        "b": (0.3 * n((N, 1))).astype(np.float32),
        "gate": np.tile(np.random.uniform(0.5, 1.5, (D, 1, V)), (1, P, 1)).astype(ml_dtypes.bfloat16).astype(np.float32),
        "offs": striped(np.concatenate([np.random.permutation(T)[:V] for _ in range(D)])),
    }


def reference(xT, w_words, w_scales, b, gate, offs):
    w = unpack_weight(w_words, w_scales)
    idx = unstriped(offs)
    x = sum(f64(gate)[d, :1] * f64(xT)[:, idx[d * V:(d + 1) * V]] for d in range(D))
    return gelu((w.T @ mxq(x, 0, "e4m3")) + f64(b))

@@ -1,0 +1,197 @@
+from contextlib import ExitStack
+
+import concourse.mybir as mybir
+from concourse.masks import make_identity
+
+K, T, D, V, N = 1024, 2048, 3, 256, 512
+S = D * V
+FLOPS = 2 * K * N * V
+
+F32 = mybir.dt.float32
+BF16 = mybir.dt.bfloat16
+I32 = mybir.dt.int32
+U32 = mybir.dt.uint32
+U16 = mybir.dt.uint16
+U8 = mybir.dt.uint8
+FP8X4 = mybir.dt.float8_e4m3fn_x4
+MULT = mybir.AluOpType.mult
+ADD = mybir.AluOpType.add
+GELU = mybir.ActivationFunctionType.Gelu_apprx_tanh
+
+P = 128
+PACK = 4
+PASSES = K // (P * PACK)
+HALF = V // 2
+M_TILES = N // P
+BANK = 512
+
+
+def tile_picked_bag_lin_gelu_sub_l_kernel(tc, xT, w_words, w_scales, b, gate, offs, out):
+    nc = tc.nc
+    with ExitStack() as ctx:
+        keep = ctx.enter_context(tc.tile_pool(name="keep", bufs=1))
+        ring = ctx.enter_context(tc.tile_pool(name="ring", bufs=2))
+        psum = ctx.enter_context(tc.psum_pool(name="psum", bufs=1))
+
+        def bank(j):
+            return psum.tile([P, BANK], F32, tag="bank%d" % j, name="bank%d" % j)
+
+        gate_rows = keep.tile([P, P], F32, name="gate_rows")
+        nc.sync.dma_start(gate_rows[:], gate.rearrange("d r (h v) -> (d r h) v", h=2)[0 : 5 * P : 5, :])
+        bias_rows = keep.tile([P, P], F32, name="bias_rows")
+        nc.vector.memset(bias_rows[:], 0.0)
+        offsets = keep.tile([P, S // 16], U16, name="offsets")
+        rows = xT.rearrange("(a p t) n -> a t p n", p=P, t=PACK)
+        windows = {}
+        for a in range(PASSES):
+            for t in range(PACK):
+                windows[a, t] = keep.tile([P, T], F32, name="window%d%d" % (a, t))
+                nc.sync.dma_start(windows[a, t][:], rows[a, t])
+                if (a, t) == (0, 0):
+                    nc.sync.dma_start(offsets[:], offs)
+                if (a, t) == (0, 1):
+                    nc.sync.dma_start(bias_rows[0:M_TILES, :], b.rearrange("(j m) o -> j (m o)", j=M_TILES))
+
+        w_scale = keep.tile([P, PASSES, N], U8, name="w_scale", align_bytes=64)
+        nc.vector.memset(w_scale[:].rearrange("p a m -> p (a m)").bitcast(I32), 0)
+        for q in range(4):
+            nc.sync.dma_start(
+                w_scale[32 * q : 32 * q + 4, :, :].bitcast(I32),
+                w_scales[:, 4 * q : 4 * q + 4, :].rearrange("a r m -> r a m").bitcast(I32),
+            )
+        w_code = keep.tile([P, PASSES, N], I32, name="w_code", align_bytes=64)
+        for a in range(PASSES):
+            nc.sync.dma_start(w_code[:, a, :], w_words[a].rearrange("p m r -> p (m r)").bitcast(I32))
+
+        ident = keep.tile([P, P], F32, name="ident")
+        make_identity(nc, ident[:])
+
+        warm = keep.tile([P, 1], F32, name="warm")
+        nc.scalar.activation(warm[:], ident[:, 0:1], GELU)
+
+        turned = bank(0)
+        nc.tensor.transpose(turned[:, 0:P], gate_rows[:], ident[:])
+        cols = keep.tile([P, P], F32, name="cols")
+        nc.scalar.copy(cols[:], turned[:, 0:P])
+        gates = keep.tile([P, S], F32, name="gates")
+        for d in range(D):
+            spread = bank(1 + d)
+            for h in range(2):
+                nc.tensor.transpose(spread[:, h * HALF : (h + 1) * HALF], cols[:, 52 * d + h : 52 * d + h + 1].to_broadcast([P, P]), ident[:])
+            nc.scalar.copy(gates[:, d * V : (d + 1) * V], spread[:, 0:V])
+        turned_bias = bank(4)
+        nc.tensor.transpose(turned_bias[:, 0:P], bias_rows[:], ident[:])
+        bias = keep.tile([P, M_TILES], F32, name="bias")
+        nc.scalar.copy(bias[:], turned_bias[:, 0:M_TILES])
+
+        x_bf = [keep.tile([P, V, PACK], BF16, name="x_bf%d" % a, align_bytes=64) for a in range(PASSES)]
+        x_code = [keep.tile([P, V], U32, name="x_code%d" % a, align_bytes=64) for a in range(PASSES)]
+        x_scale = [keep.tile([P, V], U8, name="x_scale%d" % a, align_bytes=64) for a in range(PASSES)]
+
+        def gather(dst, window, lo, n):
+            nc.vector.tensor_tensor(
+                dst[:, lo : lo + n],
+                window[:].indirect(offsets[:, lo // 16 : (lo + n) // 16]),
+                gates[:, lo : lo + n],
+                MULT,
+            )
+
+        def quantize(a, lo, n):
+            nc.vector.quantize_mx(
+                out=x_code[a][:, lo : lo + n].bitcast(FP8X4),
+                scales=x_scale[a][:, lo : lo + n],
+                in_=x_bf[a][:, lo : lo + n, :].rearrange("p v t -> p (v t)"),
+            )
+
+        step = 0
+        for a, u in ((0, 0), (0, 1), (1, 0)):
+            back = bank(2 + step // 2 % 2)
+            for e in range(2):
+                picked = ring.tile([P, S], F32, name="picked")
+                if step == 0:
+                    for d in range(D):
+                        gather(picked, windows[a, 2 * u + e], d * V, V)
+                else:
+                    gather(picked, windows[a, 2 * u + e], 0, S)
+                acc = bank(step % 2)
+                for h in range(2):
+                    for d in range(D):
+                        lo = d * V + h * HALF
+                        nc.tensor.matmul(
+                            acc[:, h * P : (h + 1) * P],
+                            lhsT=picked[:, lo : lo + HALF],
+                            rhs=ident[:],
+                            start=(d == 0),
+                            stop=(d == D - 1),
+                            is_transpose=True,
+                        )
+                sums = ring.tile([P, 2 * P], F32, name="sums")
+                nc.scalar.copy(sums[:], acc[:, 0 : 2 * P])
+                for h in range(2):
+                    lo = e * V + h * HALF
+                    nc.tensor.transpose(back[:, lo : lo + HALF], sums[:, h * P : (h + 1) * P], ident[:])
+                step += 1
+            nc.scalar.copy(x_bf[a][:, :, 2 * u : 2 * u + 2], back[:].rearrange("p (e v) -> p v e", e=2))
+            if (a, u) == (0, 1):
+                quantize(0, 0, V)
+
+        a = PASSES - 1
+        last = keep.tile([P, 2, S], F32, name="last")
+        part = keep.tile([P, 2, V], F32, name="part")
+        full = keep.tile([P, 2, HALF], F32, name="full")
+        gather(last[:, 0, :], windows[a, 2], 0, S)
+        nc.vector.tensor_tensor(part[:, 0, :], last[:, 0, 0:V], last[:, 0, V : 2 * V], ADD)
+        nc.vector.tensor_tensor(full[:, 0, :], part[:, 0, 0:HALF], last[:, 0, 2 * V : 2 * V + HALF], ADD)
+
+        groups = {}
+        for h in range(2):
+            for m in range(M_TILES):
+                groups[m, h] = bank(h * M_TILES + m)
+
+        def product(a, m, h):
+            nc.tensor.matmul_mx(
+                out=groups[m, h][:, 0:HALF],
+                lhsT=w_code[:, a, m * P : (m + 1) * P].bitcast(FP8X4),
+                lhsT_scale=w_scale[:, a, m * P : (m + 1) * P],
+                rhs=x_code[a][:, h * HALF : (h + 1) * HALF].bitcast(FP8X4),
+                rhs_scale=x_scale[a][:, h * HALF : (h + 1) * HALF],
+                start=(a == 0),
+                stop=(a == PASSES - 1),
+            )
+
+        for h in range(2):
+            for m in range(M_TILES):
+                product(0, m, h)
+
+        result = keep.tile([P, 2, M_TILES, HALF], F32, name="result")
+        win = windows[a, 3]
+        mine = last[:, 1, :]
+        lo0, lo1 = slice(0, HALF), slice(HALF, V)
+        for d in range(D):
+            gather(mine, win, d * V, HALF)
+        nc.vector.tensor_tensor(part[:, 1, lo0], mine[:, 0:HALF], mine[:, V : V + HALF], ADD)
+        gather(mine, win, HALF, HALF)
+        nc.vector.tensor_tensor(full[:, 1, :], part[:, 1, lo0], mine[:, 2 * V : 2 * V + HALF], ADD)
+        nc.scalar.copy(x_bf[a][:, lo0, 2:4], full[:].rearrange("p e v -> p v e"))
+        gather(mine, win, V + HALF, HALF)
+        gather(mine, win, 2 * V + HALF, HALF)
+        nc.vector.tensor_tensor(part[:, 1, lo1], mine[:, HALF:V], mine[:, V + HALF : 2 * V], ADD)
+        quantize(a, 0, HALF)
+        nc.vector.tensor_tensor(
+            x_bf[a][:, lo1, 2:4],
+            part[:, :, lo1].rearrange("p e v -> p v e"),
+            last[:, :, 2 * V + HALF : S].rearrange("p e v -> p v e"),
+            ADD,
+        )
+        quantize(a, HALF, HALF)
+
+        tiles = out.rearrange("(m p) v -> p m v", p=P)
+        for h in range(2):
+            for m in range(M_TILES):
+                product(a, m, h)
+            for m in range(M_TILES):
+                nc.scalar.activation(result[:, h, m, :], groups[m, h][:, 0:HALF], GELU, bias=bias[:, m : m + 1])
+                if h == 1:
+                    nc.sync.dma_start(tiles[:, m, HALF:V], result[:, h, m, :])
+            if h == 0:
+                nc.sync.dma_start(tiles[:, :, 0:HALF], result[:, h, :, :])

@@ -37,7 +37,9 @@ def tile_picked_bag_lin_gelu_sub_l_kernel(tc, xT, w_words, w_scales, b, gate, of
             return psum.tile([P, BANK], F32, tag="bank%d" % j, name="bank%d" % j)
 
         gate_rows = keep.tile([P, P], F32, name="gate_rows")
-        nc.sync.dma_start(gate_rows[:], gate.rearrange("d r (h v) -> (d r h) v", h=2)[0 : 5 * P : 5, :])
+        nc.sync.dma_start(gate_rows[0:32, :], gate.rearrange("d r (h v) -> (d r h) v", h=2)[0 : 23 * 32 : 23, :])
+        nc.vector.memset(gate_rows[32:64, :], 0.0)
+        nc.vector.memset(gate_rows[64:P, :], 0.0)
         bias_rows = keep.tile([P, P], F32, name="bias_rows")
         nc.vector.memset(bias_rows[:], 0.0)
         offsets = keep.tile([P, S // 16], U16, name="offsets")
@@ -45,7 +47,7 @@ def tile_picked_bag_lin_gelu_sub_l_kernel(tc, xT, w_words, w_scales, b, gate, of
         windows = {}
         for a in range(PASSES):
             for t in range(PACK):
-                windows[a, t] = keep.tile([P, T], F32, name="window%d%d" % (a, t))
+                windows[a, t] = keep.tile([P, T], F32, name="window%d%d" % (a, t), tag="window%d%d" % (a, t), align_bytes=64)
                 nc.sync.dma_start(windows[a, t][:], rows[a, t])
                 if (a, t) == (0, 0):
                     nc.sync.dma_start(offsets[:], offs)
@@ -59,9 +61,9 @@ def tile_picked_bag_lin_gelu_sub_l_kernel(tc, xT, w_words, w_scales, b, gate, of
                 w_scale[32 * q : 32 * q + 4, :, :].bitcast(I32),
                 w_scales[:, 4 * q : 4 * q + 4, :].rearrange("a r m -> r a m").bitcast(I32),
             )
-        w_code = keep.tile([P, PASSES, N], I32, name="w_code", align_bytes=64)
+        w_code = [keep.tile([P, N], I32, name="w_code%d" % a, align_bytes=64) for a in range(PASSES)]
         for a in range(PASSES):
-            nc.sync.dma_start(w_code[:, a, :], w_words[a].rearrange("p m r -> p (m r)").bitcast(I32))
+            nc.sync.dma_start(w_code[a][:], w_words[a].rearrange("p m r -> p (m r)").bitcast(I32))
 
         ident = keep.tile([P, P], F32, name="ident")
         make_identity(nc, ident[:])
@@ -71,26 +73,26 @@ def tile_picked_bag_lin_gelu_sub_l_kernel(tc, xT, w_words, w_scales, b, gate, of
 
         turned = bank(0)
         nc.tensor.transpose(turned[:, 0:P], gate_rows[:], ident[:])
-        cols = keep.tile([P, P], F32, name="cols")
-        nc.scalar.copy(cols[:], turned[:, 0:P])
+        cols = keep.tile([P, D, 2], F32, name="cols")
+        nc.scalar.copy(cols[:], turned[:, 0 : D * 12].rearrange("p (d c) -> p d c", d=D)[:, :, 0:2])
         gates = keep.tile([P, S], F32, name="gates")
-        for d in range(D):
-            spread = bank(1 + d)
-            for h in range(2):
-                nc.tensor.transpose(spread[:, h * HALF : (h + 1) * HALF], cols[:, 52 * d + h : 52 * d + h + 1].to_broadcast([P, P]), ident[:])
-            nc.scalar.copy(gates[:, d * V : (d + 1) * V], spread[:, 0:V])
-        turned_bias = bank(4)
-        nc.tensor.transpose(turned_bias[:, 0:P], bias_rows[:], ident[:])
+        for h in range(2):
+            spread = bank(1 + h)
+            for d in range(D):
+                nc.tensor.transpose(spread[:, d * HALF : (d + 1) * HALF], cols[:, d, h : h + 1].to_broadcast([P, P]), ident[:])
+            nc.scalar.copy(
+                gates[:].rearrange("p (d h v) -> p h d v", d=D, h=2)[:, h],
+                spread[:, 0 : D * HALF].rearrange("p (d v) -> p d v", d=D),
+            )
         bias = keep.tile([P, M_TILES], F32, name="bias")
-        nc.scalar.copy(bias[:], turned_bias[:, 0:M_TILES])
 
-        x_bf = [keep.tile([P, V, PACK], BF16, name="x_bf%d" % a, align_bytes=64) for a in range(PASSES)]
-        x_code = [keep.tile([P, V], U32, name="x_code%d" % a, align_bytes=64) for a in range(PASSES)]
+        x_bf = [keep.tile([P, V, PACK], BF16, name="x_bf%d" % a, tag="x_bf%d" % a, align_bytes=64) for a in range(PASSES)]
+        x_code = {1: keep.tile([P, V], U32, name="x_code1", align_bytes=64)}
         x_scale = [keep.tile([P, V], U8, name="x_scale%d" % a, align_bytes=64) for a in range(PASSES)]
 
         def gather(dst, window, lo, n):
             nc.vector.tensor_tensor(
-                dst[:, lo : lo + n],
+                dst,
                 window[:].indirect(offsets[:, lo // 16 : (lo + n) // 16]),
                 gates[:, lo : lo + n],
                 MULT,
@@ -103,55 +105,71 @@ def tile_picked_bag_lin_gelu_sub_l_kernel(tc, xT, w_words, w_scales, b, gate, of
                 in_=x_bf[a][:, lo : lo + n, :].rearrange("p v t -> p (v t)"),
             )
 
-        step = 0
-        for a, u in ((0, 0), (0, 1), (1, 0)):
-            back = bank(2 + step // 2 % 2)
+        pairs = ((0, 0), (0, 1), (1, 0))
+        acc = bank(0)
+        for a, u in pairs:
             for e in range(2):
-                picked = ring.tile([P, S], F32, name="picked")
-                if step == 0:
-                    for d in range(D):
-                        gather(picked, windows[a, 2 * u + e], d * V, V)
+                picked = ring.tile([P, S], F32, name="picked", tag="picked")
+                if (a, u, e) == (0, 0, 0):
+                    for h in range(2):
+                        for d in range(D):
+                            lo = d * V + h * HALF
+                            gather(picked[:, lo : lo + HALF], windows[a, 2 * u + e], lo, HALF)
                 else:
-                    gather(picked, windows[a, 2 * u + e], 0, S)
-                acc = bank(step % 2)
+                    gather(picked[:], windows[a, 2 * u + e], 0, S)
                 for h in range(2):
                     for d in range(D):
                         lo = d * V + h * HALF
                         nc.tensor.matmul(
-                            acc[:, h * P : (h + 1) * P],
+                            acc[:, (2 * e + h) * P : (2 * e + h + 1) * P],
                             lhsT=picked[:, lo : lo + HALF],
                             rhs=ident[:],
                             start=(d == 0),
                             stop=(d == D - 1),
                             is_transpose=True,
                         )
-                sums = ring.tile([P, 2 * P], F32, name="sums")
-                nc.scalar.copy(sums[:], acc[:, 0 : 2 * P])
-                for h in range(2):
-                    lo = e * V + h * HALF
-                    nc.tensor.transpose(back[:, lo : lo + HALF], sums[:, h * P : (h + 1) * P], ident[:])
-                step += 1
-            nc.scalar.copy(x_bf[a][:, :, 2 * u : 2 * u + 2], back[:].rearrange("p (e v) -> p v e", e=2))
-            if (a, u) == (0, 1):
+            if (a, u) == pairs[-1]:
+                x_code[0] = keep.tile([P, V], U32, name="x_code0", tag="window11", align_bytes=64)
                 quantize(0, 0, V)
+            sums = ring.tile([P, 2, P, 2], BF16, name="sums")
+            nc.scalar.copy(sums[:], acc[:].rearrange("v (e h p) -> v h p e", e=2, h=2))
+            words = sums[:].rearrange("v h p e -> v (h p e)").bitcast(F32)
+            back = bank(2 + u)
+            for h in range(2):
+                nc.tensor.transpose(back[:, h * P : (h + 1) * P], words[:, h * P : (h + 1) * P], ident[:])
+            if (a, u) != pairs[-1]:
+                acc = bank(0)
+                nc.tensor.transpose(acc[:, P // 2 : P // 2 + P], words[:, 0:P], ident[:])
+            x_words = x_bf[a][:].rearrange("p v t -> p (v t)").bitcast(F32).rearrange("p (v u) -> p v u", u=2)
+            nc.scalar.copy(x_words[:, :, u], back[:, 0:V])
+            if (a, u) == pairs[0]:
+                turned_bias = bank(2)
+                nc.tensor.transpose(turned_bias[:, 0:P], bias_rows[:], ident[:])
+                nc.scalar.copy(bias[:], turned_bias[:, 0:M_TILES])
+        for j in (0, 1, 3, 4, 5, 6, 7):
+            nc.tensor.transpose(bank(j)[:, 0:P], words[:, 0:P], ident[:])
 
         a = PASSES - 1
-        last = keep.tile([P, 2, S], F32, name="last")
-        part = keep.tile([P, 2, V], F32, name="part")
-        full = keep.tile([P, 2, HALF], F32, name="full")
-        gather(last[:, 0, :], windows[a, 2], 0, S)
-        nc.vector.tensor_tensor(part[:, 0, :], last[:, 0, 0:V], last[:, 0, V : 2 * V], ADD)
-        nc.vector.tensor_tensor(full[:, 0, :], part[:, 0, 0:HALF], last[:, 0, 2 * V : 2 * V + HALF], ADD)
+        work = ring.tile([P, 10, HALF], F32, name="work", tag="picked")
+        flat = work[:].rearrange("p s v -> p (s v)")
+
+        def add(dst, i, j):
+            nc.vector.tensor_tensor(work[:, dst, :], work[:, i, :], work[:, j, :], ADD)
+
+        gather(flat[:, V:S], windows[a, 2], 0, 2 * V)
+        gather(flat[:, 0:V], windows[a, 2], 2 * V, V)
+        add(6, 2, 4)
+        add(7, 3, 5)
 
         groups = {}
         for h in range(2):
             for m in range(M_TILES):
-                groups[m, h] = bank(h * M_TILES + m)
+                groups[m, h] = bank((h * M_TILES + m + 3) % 8)
 
         def product(a, m, h):
             nc.tensor.matmul_mx(
                 out=groups[m, h][:, 0:HALF],
-                lhsT=w_code[:, a, m * P : (m + 1) * P].bitcast(FP8X4),
+                lhsT=w_code[a][:, m * P : (m + 1) * P].bitcast(FP8X4),
                 lhsT_scale=w_scale[:, a, m * P : (m + 1) * P],
                 rhs=x_code[a][:, h * HALF : (h + 1) * HALF].bitcast(FP8X4),
                 rhs_scale=x_scale[a][:, h * HALF : (h + 1) * HALF],
@@ -165,24 +183,26 @@ def tile_picked_bag_lin_gelu_sub_l_kernel(tc, xT, w_words, w_scales, b, gate, of
 
         result = keep.tile([P, 2, M_TILES, HALF], F32, name="result")
         win = windows[a, 3]
-        mine = last[:, 1, :]
-        lo0, lo1 = slice(0, HALF), slice(HALF, V)
-        for d in range(D):
-            gather(mine, win, d * V, HALF)
-        nc.vector.tensor_tensor(part[:, 1, lo0], mine[:, 0:HALF], mine[:, V : V + HALF], ADD)
-        gather(mine, win, HALF, HALF)
-        nc.vector.tensor_tensor(full[:, 1, :], part[:, 1, lo0], mine[:, 2 * V : 2 * V + HALF], ADD)
-        nc.scalar.copy(x_bf[a][:, lo0, 2:4], full[:].rearrange("p e v -> p v e"))
-        gather(mine, win, V + HALF, HALF)
-        gather(mine, win, 2 * V + HALF, HALF)
-        nc.vector.tensor_tensor(part[:, 1, lo1], mine[:, HALF:V], mine[:, V + HALF : 2 * V], ADD)
+
+        def finish(h, parts, thirds):
+            nc.vector.tensor_tensor(
+                x_bf[a][:, h * HALF : (h + 1) * HALF, 2:4],
+                parts.rearrange("p e v -> p v e"),
+                thirds.rearrange("p e v -> p v e"),
+                ADD,
+            )
+
+        gather(work[:, 2, :], win, 0, HALF)
+        gather(work[:, 4, :], win, V, HALF)
+        gather(work[:, 3, :], win, 2 * V, HALF)
+        add(8, 2, 4)
+        gather(work[:, 5, :], win, HALF, HALF)
+        finish(0, work[:, 6:9:2, :], work[:, 0:4:3, :])
+        gather(work[:, 2, :], win, V + HALF, HALF)
         quantize(a, 0, HALF)
-        nc.vector.tensor_tensor(
-            x_bf[a][:, lo1, 2:4],
-            part[:, :, lo1].rearrange("p e v -> p v e"),
-            last[:, :, 2 * V + HALF : S].rearrange("p e v -> p v e"),
-            ADD,
-        )
+        gather(work[:, 4, :], win, 2 * V + HALF, HALF)
+        add(9, 5, 2)
+        finish(1, work[:, 7:10:2, :], work[:, 1:5:3, :])
         quantize(a, HALF, HALF)
 
         tiles = out.rearrange("(m p) v -> p m v", p=P)
@@ -191,7 +211,4 @@ def tile_picked_bag_lin_gelu_sub_l_kernel(tc, xT, w_words, w_scales, b, gate, of
                 product(a, m, h)
             for m in range(M_TILES):
                 nc.scalar.activation(result[:, h, m, :], groups[m, h][:, 0:HALF], GELU, bias=bias[:, m : m + 1])
-                if h == 1:
-                    nc.sync.dma_start(tiles[:, m, HALF:V], result[:, h, m, :])
-            if h == 0:
-                nc.sync.dma_start(tiles[:, :, 0:HALF], result[:, h, :, :])
+                nc.sync.dma_start(tiles[:, m, h * HALF : (h + 1) * HALF], result[:, h, m, :])

@@ -76,14 +76,13 @@ def tile_picked_bag_lin_gelu_sub_l_kernel(tc, xT, w_words, w_scales, b, gate, of
         cols = keep.tile([P, D, 2], F32, name="cols")
         nc.scalar.copy(cols[:], turned[:, 0 : D * 12].rearrange("p (d c) -> p d c", d=D)[:, :, 0:2])
         gates = keep.tile([P, S], F32, name="gates")
-        for h in range(2):
-            spread = bank(1 + h)
-            for d in range(D):
-                nc.tensor.transpose(spread[:, d * HALF : (d + 1) * HALF], cols[:, d, h : h + 1].to_broadcast([P, P]), ident[:])
-            nc.scalar.copy(
-                gates[:].rearrange("p (d h v) -> p h d v", d=D, h=2)[:, h],
-                spread[:, 0 : D * HALF].rearrange("p (d v) -> p d v", d=D),
-            )
+        for j, pieces in ((1, (0, 1)), (2, (2,))):
+            spread = bank(j)
+            for i, d in enumerate(pieces):
+                for h in range(2):
+                    lo = i * V + h * HALF
+                    nc.tensor.transpose(spread[:, lo : lo + HALF], cols[:, d, h : h + 1].to_broadcast([P, P]), ident[:])
+            nc.scalar.copy(gates[:, pieces[0] * V : (pieces[-1] + 1) * V], spread[:, 0 : len(pieces) * V])
         bias = keep.tile([P, M_TILES], F32, name="bias")
 
         x_bf = [keep.tile([P, V, PACK], BF16, name="x_bf%d" % a, tag="x_bf%d" % a, align_bytes=64) for a in range(PASSES)]
@@ -111,10 +110,8 @@ def tile_picked_bag_lin_gelu_sub_l_kernel(tc, xT, w_words, w_scales, b, gate, of
             for e in range(2):
                 picked = ring.tile([P, S], F32, name="picked", tag="picked")
                 if (a, u, e) == (0, 0, 0):
-                    for h in range(2):
-                        for d in range(D):
-                            lo = d * V + h * HALF
-                            gather(picked[:, lo : lo + HALF], windows[a, 2 * u + e], lo, HALF)
+                    gather(picked[:, 0 : 2 * V], windows[a, 2 * u + e], 0, 2 * V)
+                    gather(picked[:, 2 * V : S], windows[a, 2 * u + e], 2 * V, V)
                 else:
                     gather(picked[:], windows[a, 2 * u + e], 0, S)
                 for h in range(2):
@@ -150,16 +147,18 @@ def tile_picked_bag_lin_gelu_sub_l_kernel(tc, xT, w_words, w_scales, b, gate, of
             nc.tensor.transpose(bank(j)[:, 0:P], words[:, 0:P], ident[:])
 
         a = PASSES - 1
-        work = ring.tile([P, 10, HALF], F32, name="work", tag="picked")
-        flat = work[:].rearrange("p s v -> p (s v)")
+        firsts = ring.tile([P, 2 * V], F32, name="firsts", tag="picked")
+        fresh = ring.tile([P, 3 * V + HALF], F32, name="fresh", tag="picked")
+        parts = keep.tile([P, 2, V], F32, name="parts")
 
-        def add(dst, i, j):
-            nc.vector.tensor_tensor(work[:, dst, :], work[:, i, :], work[:, j, :], ADD)
+        def add_pieces(e, src):
+            for h in range(2):
+                lo = h * HALF
+                nc.vector.tensor_tensor(parts[:, e, lo : lo + HALF], src[:, lo : lo + HALF], src[:, V + lo : V + lo + HALF], ADD)
 
-        gather(flat[:, V:S], windows[a, 2], 0, 2 * V)
-        gather(flat[:, 0:V], windows[a, 2], 2 * V, V)
-        add(6, 2, 4)
-        add(7, 3, 5)
+        gather(firsts[:], windows[a, 2], 0, 2 * V)
+        gather(fresh[:, 2 * V : S], windows[a, 2], 2 * V, V)
+        add_pieces(0, firsts)
 
         groups = {}
         for h in range(2):
@@ -184,25 +183,22 @@ def tile_picked_bag_lin_gelu_sub_l_kernel(tc, xT, w_words, w_scales, b, gate, of
         result = keep.tile([P, 2, M_TILES, HALF], F32, name="result")
         win = windows[a, 3]
 
-        def finish(h, parts, thirds):
+        def finish(h, twos, thirds):
             nc.vector.tensor_tensor(
                 x_bf[a][:, h * HALF : (h + 1) * HALF, 2:4],
-                parts.rearrange("p e v -> p v e"),
+                twos.rearrange("p e v -> p v e"),
                 thirds.rearrange("p e v -> p v e"),
                 ADD,
             )
 
-        gather(work[:, 2, :], win, 0, HALF)
-        gather(work[:, 4, :], win, V, HALF)
-        gather(work[:, 3, :], win, 2 * V, HALF)
-        add(8, 2, 4)
-        gather(work[:, 5, :], win, HALF, HALF)
-        finish(0, work[:, 6:9:2, :], work[:, 0:4:3, :])
-        gather(work[:, 2, :], win, V + HALF, HALF)
+        slots = fresh[:].rearrange("p (s v) -> p s v", v=HALF)
+        gather(fresh[:, 0 : 2 * V], win, 0, 2 * V)
+        gather(slots[:, 6, :], win, 2 * V, HALF)
+        add_pieces(1, fresh)
+        finish(0, parts[:, :, 0:HALF], slots[:, 4:7:2, :])
+        gather(slots[:, 6, :], win, 2 * V + HALF, HALF)
         quantize(a, 0, HALF)
-        gather(work[:, 4, :], win, 2 * V + HALF, HALF)
-        add(9, 5, 2)
-        finish(1, work[:, 7:10:2, :], work[:, 1:5:3, :])
+        finish(1, parts[:, :, HALF:V], slots[:, 5:7, :])
         quantize(a, HALF, HALF)
 
         tiles = out.rearrange("(m p) v -> p m v", p=P)

from contextlib import ExitStack

import concourse.mybir as mybir
from concourse.masks import make_identity

K, T, D, V, N = 1024, 2048, 3, 256, 512
S = D * V
FLOPS = 2 * K * N * V

F32 = mybir.dt.float32
BF16 = mybir.dt.bfloat16
I32 = mybir.dt.int32
U32 = mybir.dt.uint32
U16 = mybir.dt.uint16
U8 = mybir.dt.uint8
FP8X4 = mybir.dt.float8_e4m3fn_x4
MULT = mybir.AluOpType.mult
ADD = mybir.AluOpType.add
GELU = mybir.ActivationFunctionType.Gelu_apprx_tanh

P = 128
PACK = 4
PASSES = K // (P * PACK)
HALF = V // 2
M_TILES = N // P
BANK = 512


def tile_picked_bag_lin_gelu_sub_l_kernel(tc, xT, w_words, w_scales, b, gate, offs, out):
    nc = tc.nc
    with ExitStack() as ctx:
        keep = ctx.enter_context(tc.tile_pool(name="keep", bufs=1))
        ring = ctx.enter_context(tc.tile_pool(name="ring", bufs=2))
        psum = ctx.enter_context(tc.psum_pool(name="psum", bufs=1))

        def bank(j):
            return psum.tile([P, BANK], F32, tag="bank%d" % j, name="bank%d" % j)

        gate_rows = keep.tile([P, P], F32, name="gate_rows")
        nc.sync.dma_start(gate_rows[0:32, :], gate.rearrange("d r (h v) -> (d r h) v", h=2)[0 : 23 * 32 : 23, :])
        nc.vector.memset(gate_rows[32:64, :], 0.0)
        nc.vector.memset(gate_rows[64:P, :], 0.0)
        bias_rows = keep.tile([P, P], F32, name="bias_rows")
        nc.vector.memset(bias_rows[:], 0.0)
        offsets = keep.tile([P, S // 16], U16, name="offsets")
        rows = xT.rearrange("(a p t) n -> a t p n", p=P, t=PACK)
        windows = {}
        for a in range(PASSES):
            for t in range(PACK):
                windows[a, t] = keep.tile([P, T], F32, name="window%d%d" % (a, t), tag="window%d%d" % (a, t), align_bytes=64)
                nc.sync.dma_start(windows[a, t][:], rows[a, t])
                if (a, t) == (0, 0):
                    nc.sync.dma_start(offsets[:], offs)
                if (a, t) == (0, 1):
                    nc.sync.dma_start(bias_rows[0:M_TILES, :], b.rearrange("(j m) o -> j (m o)", j=M_TILES))

        w_scale = keep.tile([P, PASSES, N], U8, name="w_scale", align_bytes=64)
        nc.vector.memset(w_scale[:].rearrange("p a m -> p (a m)").bitcast(I32), 0)
        for q in range(4):
            nc.sync.dma_start(
                w_scale[32 * q : 32 * q + 4, :, :].bitcast(I32),
                w_scales[:, 4 * q : 4 * q + 4, :].rearrange("a r m -> r a m").bitcast(I32),
            )
        w_code = [keep.tile([P, N], I32, name="w_code%d" % a, align_bytes=64) for a in range(PASSES)]
        for a in range(PASSES):
            nc.sync.dma_start(w_code[a][:], w_words[a].rearrange("p m r -> p (m r)").bitcast(I32))

        ident = keep.tile([P, P], F32, name="ident")
        make_identity(nc, ident[:])

        warm = keep.tile([P, 1], F32, name="warm")
        nc.scalar.activation(warm[:], ident[:, 0:1], GELU)

        turned = bank(0)
        nc.tensor.transpose(turned[:, 0:P], gate_rows[:], ident[:])
        cols = keep.tile([P, D, 2], F32, name="cols")
        nc.scalar.copy(cols[:], turned[:, 0 : D * 12].rearrange("p (d c) -> p d c", d=D)[:, :, 0:2])
        gates = keep.tile([P, S], F32, name="gates")
        for j, pieces in ((1, (0, 1)), (2, (2,))):
            spread = bank(j)
            for i, d in enumerate(pieces):
                for h in range(2):
                    lo = i * V + h * HALF
                    nc.tensor.transpose(spread[:, lo : lo + HALF], cols[:, d, h : h + 1].to_broadcast([P, P]), ident[:])
            nc.scalar.copy(gates[:, pieces[0] * V : (pieces[-1] + 1) * V], spread[:, 0 : len(pieces) * V])
        bias = keep.tile([P, M_TILES], F32, name="bias")

        x_bf = [keep.tile([P, V, PACK], BF16, name="x_bf%d" % a, tag="x_bf%d" % a, align_bytes=64) for a in range(PASSES)]
        x_code = {1: keep.tile([P, V], U32, name="x_code1", align_bytes=64)}
        x_scale = [keep.tile([P, V], U8, name="x_scale%d" % a, align_bytes=64) for a in range(PASSES)]

        def gather(dst, window, lo, n):
            nc.vector.tensor_tensor(
                dst,
                window[:].indirect(offsets[:, lo // 16 : (lo + n) // 16]),
                gates[:, lo : lo + n],
                MULT,
            )

        def quantize(a, lo, n):
            nc.vector.quantize_mx(
                out=x_code[a][:, lo : lo + n].bitcast(FP8X4),
                scales=x_scale[a][:, lo : lo + n],
                in_=x_bf[a][:, lo : lo + n, :].rearrange("p v t -> p (v t)"),
            )

        pairs = ((0, 0), (0, 1), (1, 0))
        acc = bank(0)
        for a, u in pairs:
            for e in range(2):
                picked = ring.tile([P, S], F32, name="picked", tag="picked")
                if (a, u, e) == (0, 0, 0):
                    gather(picked[:, 0 : 2 * V], windows[a, 2 * u + e], 0, 2 * V)
                    gather(picked[:, 2 * V : S], windows[a, 2 * u + e], 2 * V, V)
                else:
                    gather(picked[:], windows[a, 2 * u + e], 0, S)
                for h in range(2):
                    for d in range(D):
                        lo = d * V + h * HALF
                        nc.tensor.matmul(
                            acc[:, (2 * e + h) * P : (2 * e + h + 1) * P],
                            lhsT=picked[:, lo : lo + HALF],
                            rhs=ident[:],
                            start=(d == 0),
                            stop=(d == D - 1),
                            is_transpose=True,
                        )
            if (a, u) == pairs[-1]:
                x_code[0] = keep.tile([P, V], U32, name="x_code0", tag="window11", align_bytes=64)
                quantize(0, 0, V)
            sums = ring.tile([P, 2, P, 2], BF16, name="sums")
            nc.scalar.copy(sums[:], acc[:].rearrange("v (e h p) -> v h p e", e=2, h=2))
            words = sums[:].rearrange("v h p e -> v (h p e)").bitcast(F32)
            back = bank(2 + u)
            for h in range(2):
                nc.tensor.transpose(back[:, h * P : (h + 1) * P], words[:, h * P : (h + 1) * P], ident[:])
            if (a, u) != pairs[-1]:
                acc = bank(0)
                nc.tensor.transpose(acc[:, P // 2 : P // 2 + P], words[:, 0:P], ident[:])
            x_words = x_bf[a][:].rearrange("p v t -> p (v t)").bitcast(F32).rearrange("p (v u) -> p v u", u=2)
            nc.scalar.copy(x_words[:, :, u], back[:, 0:V])
            if (a, u) == pairs[0]:
                turned_bias = bank(2)
                nc.tensor.transpose(turned_bias[:, 0:P], bias_rows[:], ident[:])
                nc.scalar.copy(bias[:], turned_bias[:, 0:M_TILES])
        for j in (0, 1, 3, 4, 5, 6, 7):
            nc.tensor.transpose(bank(j)[:, 0:P], words[:, 0:P], ident[:])

        a = PASSES - 1
        firsts = ring.tile([P, 2 * V], F32, name="firsts", tag="picked")
        fresh = ring.tile([P, 3 * V + HALF], F32, name="fresh", tag="picked")
        parts = keep.tile([P, 2, V], F32, name="parts")

        def add_pieces(e, src):
            for h in range(2):
                lo = h * HALF
                nc.vector.tensor_tensor(parts[:, e, lo : lo + HALF], src[:, lo : lo + HALF], src[:, V + lo : V + lo + HALF], ADD)

        gather(firsts[:], windows[a, 2], 0, 2 * V)
        gather(fresh[:, 2 * V : S], windows[a, 2], 2 * V, V)
        add_pieces(0, firsts)

        groups = {}
        for h in range(2):
            for m in range(M_TILES):
                groups[m, h] = bank((h * M_TILES + m + 3) % 8)

        def product(a, m, h):
            nc.tensor.matmul_mx(
                out=groups[m, h][:, 0:HALF],
                lhsT=w_code[a][:, m * P : (m + 1) * P].bitcast(FP8X4),
                lhsT_scale=w_scale[:, a, m * P : (m + 1) * P],
                rhs=x_code[a][:, h * HALF : (h + 1) * HALF].bitcast(FP8X4),
                rhs_scale=x_scale[a][:, h * HALF : (h + 1) * HALF],
                start=(a == 0),
                stop=(a == PASSES - 1),
            )

        for h in range(2):
            for m in range(M_TILES):
                product(0, m, h)

        result = keep.tile([P, 2, M_TILES, HALF], F32, name="result")
        win = windows[a, 3]

        def finish(h, twos, thirds):
            nc.vector.tensor_tensor(
                x_bf[a][:, h * HALF : (h + 1) * HALF, 2:4],
                twos.rearrange("p e v -> p v e"),
                thirds.rearrange("p e v -> p v e"),
                ADD,
            )

        slots = fresh[:].rearrange("p (s v) -> p s v", v=HALF)
        gather(fresh[:, 0 : 2 * V], win, 0, 2 * V)
        gather(slots[:, 6, :], win, 2 * V, HALF)
        add_pieces(1, fresh)
        finish(0, parts[:, :, 0:HALF], slots[:, 4:7:2, :])
        gather(slots[:, 6, :], win, 2 * V + HALF, HALF)
        quantize(a, 0, HALF)
        finish(1, parts[:, :, HALF:V], slots[:, 5:7, :])
        quantize(a, HALF, HALF)

        tiles = out.rearrange("(m p) v -> p m v", p=P)
        for h in range(2):
            for m in range(M_TILES):
                product(a, m, h)
            for m in range(M_TILES):
                nc.scalar.activation(result[:, h, m, :], groups[m, h][:, 0:HALF], GELU, bias=bias[:, m : m + 1])
                nc.sync.dma_start(tiles[:, m, h * HALF : (h + 1) * HALF], result[:, h, m, :])
